import numpy as np, ml_dtypes
CORES = [25,29,65,69,153,157,193,197]
N = 8
BF = ml_dtypes.bfloat16
def gentries(a):
    return np.ascontiguousarray(a.reshape(8, 16, -1).transpose(0, 2, 1)).reshape(8, -1)
def gtable(e):
    e = np.asarray(e); return np.ascontiguousarray(e.reshape(8, -1, 16).transpose(0, 2, 1)).reshape(128, -1).astype(np.int32)
V, R = 2048, 3
def family(rng, sizes, depth, pool, mix, fall=None):
    key = np.tile(np.arange(V), (N, 1)); lev = np.zeros(V, np.int64); comp = np.zeros(V, np.int64); via = [-1] * V; o = rng.permutation(V); a = 0
    for i in range(len(sizes)):
        s, D = int(sizes[i]), int(depth[i]); m = o[a:a + s]; a += s; comp[m] = i
        if s == 1: continue
        root = int(np.min(m)); m = m[m != root]; l = np.concatenate([np.arange(1, D + 1), rng.integers(1, D + 1, s - 1 - D)])
        if fall is not None and fall[i]: m = np.sort(m)[::-1]; l = np.sort(l)
        lev[m] = l
        at = [[root]] + [[] for k in range(D)]
        for c, k in zip(m.tolist(), l.tolist()): at[k].append(c)
        for k in range(1, D + 1):
            for c in at[k]:
                p = at[k - 1][int(rng.integers(len(at[k - 1])))]; w = [q for q in pool if q != via[p]]; q = w[int(rng.integers(len(w)))]
                key[q, c] = key[q, p]; via[c] = q
    for q in range(N if mix > 0 else 0):
        h = np.flatnonzero(key[q] == np.arange(V)); t = comp[h] * (R + 1) + lev[h]; keep = rng.random(h.size) >= mix
        hk, tk = h[keep], t[keep]; s = np.argsort(tk, kind="stable"); hk, tk = hk[s], tk[s]
        lo = np.searchsorted(tk, t, "left"); n = np.searchsorted(tk, t, "right") - lo; z = ~keep & (n > 0)
        to = h + 0; to[z] = hk[lo[z] + (rng.random(np.count_nonzero(z)) * n[z]).astype(np.int64)]
        jump = np.arange(V); jump[h] = to; key[q] = jump[key[q]]
    return key
def lay(rng, key, way):
    if way == 0: o = np.lexsort((rng.random(V), rng.permutation(V)[key]))
    elif way == 1: o = np.lexsort((np.arange(V), key))
    else: o = np.lexsort((-np.arange(V), -key))
    k = key[o]; s = np.ones(V, np.int64); s[1:] = k[1:] != k[:-1]
    e = np.append(np.flatnonzero(s)[1:], V) - 1; last = np.zeros(V, np.int64); last[o] = e[np.add.accumulate(s) - 1]
    return [o, s, last]
def pack(rng, keys, ways):
    a = np.array([[lay(rng, keys[g][q], ways[q, g]) for g in range(8)] for q in range(N)])
    return {"pm": np.stack([gtable(u) for u in a[:, :, 0]]), "en": np.stack([gtable(u) for u in a[:, :, 2]]), "st": np.ascontiguousarray(a[:, :, 1]).astype(np.int32)}
def depths(rng, s):
    top = np.minimum(R, s - 1); D = np.where(top > 0, 1 + (rng.random(s.size) * top).astype(np.int64), 0); i = np.argmax(s); D[i] = top[i]; return D
def some(rng):
    out = []
    for n in rng.choice(np.arange(6, 41), 8, replace=False):
        c = np.sort(rng.choice(V - 1, int(n) - 1, replace=False)) + 1; s = np.diff(np.concatenate([[0], c, [V]]))
        out.append(family(rng, s, depths(rng, s), list(range(N)), rng.choice([0.0, 0.05, 0.15])))
    return out
def setup_inputs(rng):
    return pack(rng, some(rng), np.zeros((N, 8), np.int64))
def setup_inputs_deep(rng):
    few = rng.permutation(8)[:4]; n = rng.choice(np.arange(V // (2 * (R + 1)), V // (R + 1) + 1), 8, replace=False); keys = []
    for g in range(8):
        m = int(n[g]); s = [R + 1] * m + [1] * (V - m * (R + 1)); pool = rng.permutation(N)[:2].tolist() if g in few else list(range(N))
        keys.append(family(rng, s, [R] * m + [0] * (V - m * (R + 1)), pool, 0.0, np.arange(len(s)) % 2 == 0))
    return pack(rng, keys, np.zeros((N, 8), np.int64))
def setup_inputs_ends(rng):
    keys = some(rng); w = rng.permutation(8); one = np.tile(np.arange(V), (N, 1))
    keys[w[0]][rng.integers(N)] = 0
    keys[w[1]] = one + 0
    keys[w[2]] = np.tile(rng.integers(0, 30, V), (N, 1))
    keys[w[3]] = one + 0; keys[w[3]][rng.integers(N)] = rng.integers(0, 3, V)
    x = np.concatenate([[0], 1 + rng.choice(V - 2, R - 1, replace=False), [V - 1]]); k = one + 0; ab = rng.permutation(N)[:2]
    for i in range(R): k[ab[i % 2], x[i + 1]] = x[i]
    keys[w[4]] = k
    return pack(rng, keys, np.zeros((N, 8), np.int64))
def setup_inputs_order(rng):
    return pack(rng, some(rng), rng.integers(1, 3, (N, 8)))
def setup_inputs_spread(rng):
    keys = []; half = int(rng.integers(8))
    for g in range(8):
        s = [1] * (V // 2 if g == half else 0); left = V - len(s)
        while left > 0:
            t = max(1, int(left * (0.3 + 0.4 * rng.random()))); s.append(t); left -= t
        s = np.array(s); keys.append(family(rng, s, depths(rng, s), list(range(N)) + [int(rng.integers(N))] * (3 * N), rng.choice([0.0, 0.3, 0.8])))
    return pack(rng, keys, np.zeros((N, 8), np.int64))
def hop(p, st, L):
    g = np.arange(8)[:, None]; M = L
    for q in range(N):
        s = st[q].reshape(-1); m = np.minimum.reduceat(L[g, p[q]].reshape(-1), np.flatnonzero(s))
        u = np.empty_like(L); u[g, p[q]] = m[np.add.accumulate(s) - 1].reshape(8, V); M = np.minimum(M, u)
    return M
def check_inputs(d):
    p = np.stack([gentries(a) for a in d["pm"]]); e = np.stack([gentries(a) for a in d["en"]]); s = d["st"]
    if not (np.sort(p, -1) == np.arange(V)).all(): return ["pm: every vertex once"]
    if not (((s == 0) | (s == 1)).all() and (s[:, :, 0] == 1).all()): return ["st: 0 and 1, beginning with 1"]
    bad = []; t = s.reshape(-1); last = ((np.append(np.flatnonzero(t)[1:], t.size) - 1) % V)[np.add.accumulate(t) - 1].reshape(N, 8, V)
    if not (np.take_along_axis(e, p, 2) == last).all(): bad.append("en: last places")
    L = np.tile(np.arange(V), (8, 1))
    for i in range(R): L = hop(p, s, L)
    if not (hop(p, s, L) == L).all(): bad.append("at most R steps to the smallest vertex")
    return bad
def reference(pm, en, st):
    p = np.stack([gentries(a) for a in pm]); L = np.tile(np.arange(V), (8, 1))
    while True:
        M = hop(p, st, L)
        if (M == L).all(): break
        L = M
    c = np.count_nonzero(L == np.arange(V), axis=1).reshape(8, 1)
    return {"y": np.stack([L[:, r * 256:(r + 1) * 256] for r in range(N)]).astype(np.float32), "cnt": np.stack([c for r in range(N)]).astype(np.float32)}

from concourse.bass import DstId, RemoteDMATransfer
from concourse.mybir import AluOpType as A, ActivationFunctionType as F

V = 2048
XA, XB = 768, 1472
SC = 2.0 ** -15
BASE = [-16384, -8192, -4096, -2048, -1024, -512, -256, -128, 0, 128, 256, 512, 1024, 2048, 4096, 8192]
SLOPE = [64, 32, 16, 8, 4, 2, 1, 1, 1, 1, 2, 4, 8, 16, 32, 64]
KNOTS = [256, 512, 1024, 2048, 4096, 8192]
WEIGHT = [2.0 ** (14 - j) for j in range(6)] + [2.0 ** 9]

SCRATCH = {
    "pmi": ("sbuf", [128, 128], "int32"), "eni": ("sbuf", [128, 128], "int32"),
    "w1p": ("sbuf", [128, 128], "uint16"), "w1e": ("sbuf", [128, 128], "uint16"),
    "w2p": ("sbuf", [128, 128], "uint16"), "w2e": ("sbuf", [128, 128], "uint16"),
    "p2i": ("sbuf", [128, 128], "int32"), "e2i": ("sbuf", [128, 128], "int32"),
    "first": ("sbuf", [128, V], "bfloat16"),
    "base": ("sbuf", [128, 128], "bfloat16"), "ones": ("sbuf", [128, 128], "bfloat16"),
    "ident": ("sbuf", [128, 128], "bfloat16"), "pick": ("sbuf", [128, 8], "bfloat16"),
    "reset": ("sbuf", [128, 128], "bfloat16"), "keep": ("sbuf", [128, 128], "bfloat16"),
    "wid": ("sbuf", [128, 7 * 128], "bfloat16"), "own": ("sbuf", [128, 128], "bfloat16"),
    "pint": ("sbuf", [128, 16], "int32"), "pmod": ("sbuf", [128, 16], "int32"), "phalf": ("sbuf", [128, 16], "int32"),
    "podd": ("sbuf", [128, 16], "int32"), "psum2": ("sbuf", [128, 16], "int32"),
    "off1": ("sbuf", [128, 10], "uint16"), "off8": ("sbuf", [128, 10], "uint16"), "offy": ("sbuf", [128, 2], "uint16"),
    "win1": ("sbuf", [128, V], "bfloat16"), "win2": ("sbuf", [128, V], "bfloat16"), "win3": ("sbuf", [128, V], "bfloat16"),
    "x1": ("sbuf", [128, V], "bfloat16"), "x2": ("sbuf", [128, V], "bfloat16"), "x3": ("sbuf", [128, V], "bfloat16"),
    "s1": ("sbuf", [128, V], "bfloat16"), "s2": ("sbuf", [128, V], "bfloat16"), "s3": ("sbuf", [128, V], "bfloat16"),
    "u1": ("sbuf", [128, V], "bfloat16"), "u2": ("sbuf", [128, V], "bfloat16"), "u3": ("sbuf", [128, V], "bfloat16"),
    "mine": ("sbuf", [128, 128], "bfloat16"), "landd": ("sbuf", [128, 48], "bfloat16"), "landr": ("sbuf", [128, 64], "bfloat16"),
    "ea": ("sbuf", [128, 32], "bfloat16"), "ra": ("sbuf", [128, 32], "bfloat16"), "rb": ("sbuf", [128, 32], "bfloat16"),
    "m1": ("sbuf", [128, 16], "bfloat16"), "m2": ("sbuf", [128, 128], "bfloat16"), "m3": ("sbuf", [128, 128], "bfloat16"),
    "b1": ("sbuf", [128, 144], "bfloat16"), "b2": ("sbuf", [128, 144], "bfloat16"),
    "ytile": ("sbuf", [128, 16], "bfloat16"), "landy": ("sbuf", [128, 128], "bfloat16"),
    "cl": ("sbuf", [128, 7 * 16], "bfloat16"), "eq": ("sbuf", [128, 128], "bfloat16"),
    "yrow": ("sbuf", [128, 128], "float32"), "crun": ("sbuf", [128, 128], "float32"), "crow": ("sbuf", [128, 8], "float32"),
    "hu": ("sbuf", [128, 32], "bfloat16"), "hy": ("sbuf", [128, 16], "bfloat16"),
    "lp": ("dram", [8, 128, 16], "int32"), "le": ("dram", [8, 128, 16], "int32"), "ls": ("dram", [8, 128, 16], "int32"),
    "dp": ("dram", [8, 128, 16], "int32"), "de": ("dram", [8, 128, 16], "int32"), "ds": ("dram", [8, 128, 16], "int32"),
    "hp": ("dram", [2, 128, 16], "int32"), "he": ("dram", [2, 128, 16], "int32"), "hs": ("dram", [2, 128, 16], "int32"),
    "psb": ("psum", [128, V], "float32"),
    "ps1": ("psum", [128, 512], "float32"), "ps2": ("psum", [128, 512], "float32"), "ps3": ("psum", [128, 512], "float32"),
    "psy": ("psum", [128, 512], "float32"),
}
NT = 128
SEMAPHORES = ["t%d" % i for i in range(NT)] + ["alist", "astart", "adir", "arel", "aydir", "ayrel", "hlist", "hstart", "hlab", "hfin"]


def runner(g, T):
    Q = {"g": g, "v": g.vector, "s": g.scalar, "p": g.tensor, "y": g.sync}
    tags, know, count = {}, {k: set() for k in Q}, [0]

    def tag(name, sem=None, n=0):
        if name not in tags:
            if sem is None:
                sem = "t%d" % count[0]
                count[0] += 1
            tags[name] = {"sem": sem, "n": n, "know": set(), "waited": False}
        return tags[name]

    def wait(q, after):
        for a in after:
            if a in know[q]:
                continue
            t = tags[a]
            Q[q].wait_ge(T.sem[t["sem"]], t["n"])
            t["waited"] = True
            know[q] |= {a} | t["know"]

    def raised(q, name, n):
        t = tag(name)
        assert not t["waited"], name
        t["n"] += n
        t["know"] |= know[q]
        return T.sem[t["sem"]]

    def op(q, name, after, call, n=1, **kw):
        wait(q, after)
        call(**kw).then_inc(raised(q, name, n), n)

    def dma(q, name, after, out, in_):
        wait(q, after)
        Q[q].dma_start(out=out, in_=in_).then_inc(raised(q, name, 16), 16)

    def send(name, after, jobs, rsem, topo, core):
        wait("g", after)
        tr, total = [], 0
        for dst, out, src, eng in jobs:
            rid, pid = topo.addr(dst, core)
            tr.append(RemoteDMATransfer(dst_ids=[DstId(rid=rid, pnc=pid)], dma_engine_mask=sum(1 << e for e in eng),
                                        remote_sem=T.sem[rsem], src=src, dst=out))
            total += len(eng)
        g.remote_dma_fused(tr, local_sem=raised("g", name, total))

    def finish():
        wait("g", [a for a in tags if not tags[a]["waited"]])

    return {"tag": tag, "wait": wait, "op": op, "dma": dma, "send": send, "finish": finish}


def plan(T, topo):
    cores = T.cores
    near = [[p for p in range(len(cores)) if cores[p] in topo.cores_of(cores[q]) or topo.same_plane(cores[q], cores[p])]
            for q in range(len(cores))]
    owners = near[0] + [p for p in range(len(cores)) if p not in near[0]]
    group = {p: k for k, p in enumerate(owners)}
    return cores, near, owners, group


def helpers(T, topo, q, far):
    c = T.cores[q]
    return [h for h in topo.cores_of(c) if T.rank_of(h) is None and topo.die(h) == topo.die(c)
            and all(topo.may_write(h, T.cores[d]) for d in far)][:2]


def helper_program(g, core, T, topo, q, far, mine):
    r = runner(g, T)
    cores, near, owners, group = plan(T, topo)
    dst = [cores[d] for d in mine]
    e = topo.engines(core, dst[0])
    slot = near[mine[0]]
    fr = [p for p in range(len(cores)) if p not in slot]
    s = fr.index(q)
    h = len(e) // 2
    k = len(e) // 4
    r["tag"]("hlist", "hlist", 4)
    r["tag"]("hstart", "hstart", 4)
    r["tag"]("hlab", "hlab", 8)
    r["tag"]("hfin", "hfin", 8)
    jobs = []
    for i in range(2):
        jobs.append((dst[i], T.dp[q], T.hp[i], e[2 * i * k:(2 * i + 1) * k]))
        jobs.append((dst[i], T.de[q], T.he[i], e[(2 * i + 1) * k:(2 * i + 2) * k]))
    r["send"]("fl", ["hlist"], jobs, "alist", topo, core)
    r["send"]("fs", ["hstart"], [(dst[i], T.ds[q], T.hs[i], e[h * i:h * i + h]) for i in range(2)], "astart", topo, core)
    r["send"]("fu", ["hlab"], [(dst[i], T.landr[:, 16 * s:16 * s + 16], T.hu[:, 16 * i:16 * i + 16], e[h * i:h * i + h])
                               for i in range(2)], "arel", topo, core)
    r["send"]("fy", ["hfin"], [(dst[i], T.landy[:, 16 * group[q]:16 * group[q] + 16], T.hy[:], e[h * i:h * i + h])
                               for i in range(2)], "ayrel", topo, core)
    r["finish"]()


def rank_program(g, core, T, topo):
    cores, near, owners, group = plan(T, topo)
    rank = T.rank_of(core)
    if rank is None:
        for q in range(len(cores)):
            if core in topo.cores_of(cores[q]):
                far = [d for d in owners if d not in near[q]]
                hs = helpers(T, topo, q, far)
                if core in hs:
                    i = hs.index(core)
                    helper_program(g, core, T, topo, q, far, far[2 * i:2 * i + 2])
        return
    R = runner(g, T)
    op, dma, send, tag, wait = R["op"], R["dma"], R["send"], R["tag"], R["wait"]
    v, s, p = g.vector, g.scalar, g.tensor
    go = group[rank]
    far = [d for d in owners if d not in near[rank]]
    hs = helpers(T, topo, rank, far)
    mate = [d for d in near[rank] if d != rank and cores[d] in topo.cores_of(core)][0]
    plane = [d for d in near[rank] if d != rank and d != mate]
    off = topo.engines(core, cores[plane[0]])
    allr = topo.engines(core, hs[0])
    on = [x for x in allr if x not in off]
    for nm, n in (("alist", 24), ("astart", 24), ("adir", 16), ("arel", 16), ("aydir", 16), ("ayrel", 16)):
        tag(nm, nm, n)

    def slot(d):
        return [x for x in near[d] if x != d].index(rank)

    dma("y", "pm", [], T.pmi[:], T.pm[:])
    dma("s", "en", [], T.eni[:], T.en[:])
    dma("y", "lpe", [], T.lp[:], T.pm[:])
    dma("s", "lpe", [], T.le[:], T.en[:])
    dma("y", "ls", [], T.ls[:], T.st[:])
    dma("y", "ownl", [], T.dp[rank], T.pm[16 * go:16 * go + 16, :])
    dma("y", "ownl", [], T.de[rank], T.en[16 * go:16 * go + 16, :])
    dma("y", "owns", [], T.ds[rank], T.st[go:go + 1, :])

    op("g", "base", [], g.iota, out=T.base[:], pattern=[[1, 128]], base=0, channel_multiplier=0,
       allow_small_or_imprecise_dtypes=True)
    op("v", "mfirst", [], v.memset, ap=T.first[:], constant=0.0)
    op("v", "ones", [], v.memset, ap=T.ones[:], constant=1.0)
    wait("g", ["mfirst"])
    dma("g", "d1", ["mfirst"], T.first[0:128:16, :], T.st[:])
    for i in range(16):
        o = T.win1[:, 128 * i:128 * i + 128]
        if i % 8 < 5:
            op("v", "win1", ["base"], v.tensor_scalar, out=o, in0=T.base[:], scalar1=SLOPE[i] * SC, scalar2=BASE[i] * SC,
               op0=A.mult, op1=A.add)
        else:
            op("s", "win1", ["base"], s.activation, out=o, in_=T.base[:], func=F.Identity, scale=SLOPE[i] * SC, bias=0.0) \
                if BASE[i] == 0 else op("s", "win1", ["base"], s.activation, out=o, in_=T.base[:], func=F.Copy,
                                        scale=SLOPE[i] * SC, bias=BASE[i] * SC)
    op("g", "pick", ["ones"], g.affine_select, out=T.pick[:], in_=T.ones[:, 0:8], pattern=[[-16, 8]], compare_op=A.is_equal,
       fill=0.0, base=0, channel_multiplier=1)
    jobs = []
    for i, d in enumerate(far):
        jobs.append((hs[i // 2], T.hp[i % 2], T.lp[group[d]], [on[2 * i]]))
        jobs.append((hs[i // 2], T.he[i % 2], T.le[group[d]], [on[2 * i + 1]]))
    direct = [(plane[0], off[0:1], off[1:2]), (plane[1], off[2:3], off[3:4]), (mate, off[4:6], off[6:8])]
    toh = jobs
    tod = []
    for d, ea, eb in direct:
        tod.append((cores[d], T.dp[rank], T.lp[group[d]], ea))
        tod.append((cores[d], T.de[rank], T.le[group[d]], eb))
    wait("g", ["lpe"])
    send_two(R, T, g, topo, core, "cl1", [(toh, "hlist"), (tod, "alist")])
    wait("g", ["ls"])
    toh = [(hs[i // 2], T.hs[i % 2], T.ls[group[d]], on[2 * i:2 * i + 2]) for i, d in enumerate(far)]
    tod = [(cores[d], T.ds[rank], T.ls[group[d]], ea + eb) for d, ea, eb in direct]
    send_two(R, T, g, topo, core, "cl2", [(toh, "hstart"), (tod, "astart")])

    def step(h, win, wp, we, ready, x, sc, u, ps, first, extra):
        n = lambda t: t + str(h)
        op("v", n("ga"), ready + [wp[1]], v.tensor_copy, out=x[:, 0:XA], in_=win[:, 0:V].indirect(wp[0][:, 0:XA // 16]))
        op("s", n("gb"), ready + [wp[1]], s.activation, out=x[:, XA:XB], in_=win[:, 0:V].indirect(wp[0][:, XA // 16:XB // 16]),
           func=F.Copy)
        op("s", n("gc"), ready, s.activation, out=x[:, XB:V], in_=win[:, 0:V].indirect(wp[0][:, XB // 16:V // 16]), func=F.Copy)
        extra()
        last = None
        for a, b, t in ((0, XA, "ga"), (XA, XB, "gb"), (XB, V, "gc")):
            op("v", n("sc" + t), [n(t), first] + ([last] if last else []), v.tensor_tensor_scan, out=sc[:, a:b],
               data0=T.first[:, a:b], data1=x[:, a:b], initial=0.0 if a == 0 else sc[:, a - 1:a], op0=A.add, op1=A.min)
            last = n("sc" + t)
        parts = (("v", 0, 768), ("s", 1024, 1792), ("v", 768, 1024), ("s", 1792, 2048))
        for q, a, b in parts:
            o, i_ = u[:, a:b], sc[:, 0:V].indirect(we[0][:, a // 16:b // 16])
            if q == "v":
                op("v", n("u%d" % a), [last, we[1]], v.tensor_copy, out=o, in_=i_)
            else:
                op("s", n("u%d" % a), [last, we[1]], s.activation, out=o, in_=i_, func=F.Copy)
        for q, a, b in parts:
            for i in range(a // 128, b // 128):
                o = ps[:, i:128:16] if h == 1 else ps[:, 8 * i:8 * i + 8]
                op("p", n("sel"), [n("u%d" % a), "pick"], p.matmul, out=o, lhsT=u[:, 128 * i:128 * i + 128], rhs=T.pick[:],
                   start=True, stop=True)

    op("v", "w1p", ["pm"], v.tensor_copy, out=T.w1p[:], in_=T.pmi[:])
    step(1, T.win1, (T.w1p, "w1p"), (T.w1e, "w1e"), ["win1"], T.x1, T.s1, T.u1, T.ps1, "d1",
         lambda: op("v", "w1e", ["en"], v.tensor_copy, out=T.w1e[:], in_=T.eni[:]))
    fa = 16 * group[far[0]]
    na = 64 - fa
    op("v", "minef", ["sel1"], v.tensor_copy, out=T.mine[:, fa:fa + 64], in_=T.ps1[:, fa:fa + 64])
    op("v", "minen", ["sel1"], v.tensor_copy, out=T.mine[:, na:na + 64], in_=T.ps1[:, na:na + 64])
    send("sf", ["minef"], [(hs[i], T.hu[:], T.mine[:, fa + 32 * i:fa + 32 * i + 32], allr[8 * i:8 * i + 8]) for i in range(2)],
         "hlab", topo, core)
    tod = [(mate, on), (plane[0], off[0:4]), (plane[1], off[4:8])]
    send("sn", ["minen"], [(cores[d], T.landd[:, 16 * slot(d):16 * slot(d) + 16],
                            T.mine[:, 16 * group[d]:16 * group[d] + 16], e) for d, e in tod], "adir", topo, core)
    dma("g", "d2", ["astart", "owns", "scgc1"], T.first[0:128:16, :], T.ds[:])
    op("g", "ident", ["ones"], g.affine_select, out=T.ident[:], in_=T.ones[:], pattern=[[-1, 128]], compare_op=A.is_equal,
       fill=0.0, base=0, channel_multiplier=1)
    op("g", "reset", ["ones"], g.affine_select, out=T.reset[:], in_=T.ones[:], pattern=[[0, 16], [1, 8]],
       compare_op=A.is_equal, fill=0.0, base=0, channel_multiplier=0)
    op("g", "pint", [], g.iota, out=T.pint[:], pattern=[[0, 16]], base=0, channel_multiplier=1)

    dma("y", "p2i", ["alist", "ownl"], T.p2i[:], T.dp[:])
    dma("y", "e2i", ["alist", "ownl"], T.e2i[:], T.de[:])
    op("v", "pmod", ["pint"], v.tensor_scalar, out=T.pmod[:], in0=T.pint[:], scalar1=15, scalar2=None, op0=A.bitwise_and)
    op("v", "off1", ["pmod"], v.tensor_scalar, out=T.off1[:], in0=T.pmod[:, 0:10], scalar1=1, scalar2=None, op0=A.mult)
    op("v", "off8", ["pmod"], v.tensor_scalar, out=T.off8[:], in0=T.pmod[:, 0:10], scalar1=8, scalar2=7, op0=A.mult, op1=A.add)
    op("v", "podd", ["pmod"], v.tensor_scalar, out=T.podd[:], in0=T.pmod[:], scalar1=1, scalar2=None, op0=A.bitwise_and)
    op("v", "phalf", ["podd"], v.tensor_scalar, out=T.phalf[:], in0=T.pmod[:], scalar1=8, scalar2=2 * rank, op0=A.mult,
       op1=A.add)
    op("v", "podd7", ["podd"], v.tensor_scalar, out=T.psum2[:], in0=T.podd[:], scalar1=7, scalar2=None, op0=A.mult)
    op("v", "podd8", ["podd7", "phalf"], v.tensor_tensor, out=T.podd[:], in0=T.phalf[:], in1=T.psum2[:], op=A.subtract)
    op("v", "offy", ["podd8"], v.tensor_scalar, out=T.offy[:], in0=T.podd[:, 0:2], scalar1=1, scalar2=None, op0=A.mult)
    op("v", "keep0", [], v.memset, ap=T.keep[:], constant=1.0)
    op("v", "keep", ["keep0"], v.memset, ap=T.keep[:, 0:128:16], constant=0.0)
    for j in range(7):
        op("s", "wid", ["ident"], s.activation, out=T.wid[:, 128 * j:128 * j + 128], in_=T.ident[:], func=F.Copy,
           scale=WEIGHT[j])
    for i in range(16):
        op("p", "qown", ["win1", "pick"], p.matmul, out=T.psy[:, i:128:16], lhsT=T.win1[:, 128 * i:128 * i + 128],
           rhs=T.pick[:], start=True, stop=True)
    op("s", "own", ["qown"], s.activation, out=T.own[:], in_=T.psy[:, 0:128], func=F.Copy)
    op("v", "w2p", ["p2i"], v.tensor_copy, out=T.w2p[:], in_=T.p2i[:])
    op("v", "w2e", ["e2i"], v.tensor_copy, out=T.w2e[:], in_=T.e2i[:])

    og = 16 * go
    op("v", "ea", ["adir"], v.tensor_tensor, out=T.ea[:, 0:16], in0=T.landd[:, 0:16], in1=T.landd[:, 16:32], op=A.min)
    op("v", "ea", ["minen"], v.tensor_tensor, out=T.ea[:, 16:32], in0=T.landd[:, 32:48], in1=T.mine[:, og:og + 16], op=A.min)
    op("v", "ra", ["arel"], v.tensor_tensor, out=T.ra[:], in0=T.landr[:, 0:32], in1=T.landr[:, 32:64], op=A.min)
    op("v", "rb", ["ra", "ea"], v.tensor_tensor, out=T.rb[:], in0=T.ra[:], in1=T.ea[:], op=A.min)
    op("v", "m1", ["rb"], v.tensor_tensor, out=T.m1[:], in0=T.rb[:, 0:16], in1=T.rb[:, 16:32], op=A.min)

    def spread(h, src, n, offs, b, win, free):
        op("v", "rep%d" % h, [src[1], offs[1]], v.tensor_copy, out=b[:], in_=src[0][:, 0:n].indirect(offs[0][:, 0:9]))
        out = []
        for k in range(4):
            for i in range(4 * k, 4 * k + 4):
                op("p", "row%d%d" % (h, k), ["rep%d" % h, "ident"] + free, p.matmul, out=T.psb[:, 128 * i:128 * i + 128],
                   lhsT=b[:, i:i + 128], rhs=T.ident[:], start=True, stop=True)
            o, i_ = win[:, 512 * k:512 * k + 512], T.psb[:, 512 * k:512 * k + 512]
            t = "w%d%d" % (h, k)
            if k % 2:
                op("v", t, ["row%d%d" % (h, k)], v.tensor_copy, out=o, in_=i_)
            else:
                op("s", t, ["row%d%d" % (h, k)], s.activation, out=o, in_=i_, func=F.Copy)
            out.append(t)
        return out

    ready = spread(2, (T.m1, "m1"), 16, (T.off1, "off1"), T.b1, T.win2, [])
    step(2, T.win2, (T.w2p, "w2p"), (T.w2e, "w2e"), ready, T.x2, T.s2, T.u2, T.ps2, "d2", lambda: None)
    op("v", "m2", ["sel2", "reset"], v.tensor_tensor_scan, out=T.m2[:], data0=T.reset[:], data1=T.ps2[:, 0:128], initial=0.0,
       op0=A.add, op1=A.min)
    ready = spread(3, (T.m2, "m2"), 128, (T.off8, "off8"), T.b2, T.win3, ready)
    step(3, T.win3, (T.w2p, "w2p"), (T.w2e, "w2e"), ready, T.x3, T.s3, T.u3, T.ps3, "d2", lambda: None)
    op("v", "m3", ["sel3"], v.tensor_tensor_scan, out=T.m3[:], data0=T.reset[:], data1=T.ps3[:, 0:128], initial=0.0,
       op0=A.add, op1=A.min)
    op("v", "yt", ["m3"], v.tensor_copy, out=T.ytile[:], in_=T.m3[:, 7:128:8])
    op("v", "yown", ["m3"], v.tensor_copy, out=T.landy[:, og:og + 16], in_=T.m3[:, 7:128:8])

    send("yf", ["yt"], [(hs[i], T.hy[:], T.ytile[:], allr[8 * i:8 * i + 8]) for i in range(2)], "hfin", topo, core)
    send("yn", ["yt"], [(cores[d], T.landy[:, og:og + 16], T.ytile[:], e) for d, e in tod], "aydir", topo, core)

    all_y = ["aydir", "ayrel", "yown"]
    for j in range(6):
        op("v", "cl", all_y + ["offy"], v.tensor_scalar, out=T.cl[:, 16 * j:16 * j + 16],
           in0=T.landy[:, 0:128].indirect(T.offy[:, 0:1]), scalar1=KNOTS[j] * SC, scalar2=-KNOTS[j] * SC, op0=A.min, op1=A.max)
    op("s", "cl", all_y + ["offy"], s.activation, out=T.cl[:, 96:112], in_=T.landy[:, 0:128].indirect(T.offy[:, 0:1]),
       func=F.Copy)
    for j in range(7):
        op("p", "psy", ["cl", "wid", "own"], p.matmul, out=T.psy[0:16, 0:128], lhsT=T.cl[:, 16 * j:16 * j + 16],
           rhs=T.wid[:, 128 * j:128 * j + 128], start=j == 0, stop=j == 6)
    op("v", "eq", all_y + ["own"], v.tensor_tensor, out=T.eq[:], in0=T.landy[:], in1=T.own[:], op=A.is_equal)
    op("p", "cnt", ["eq", "minef", "minen"], p.matmul, out=T.ps1[0:1, 0:128], lhsT=T.ones[:, 0:1], rhs=T.eq[:], start=True,
       stop=True)
    op("s", "yrow", ["psy"], s.activation, out=T.yrow[0:16, :], in_=T.psy[0:16, 0:128], func=F.Copy, bias=float(V // 2))
    dma("s", "yout", ["yrow"], T.y[:], T.yrow[0:16, :])
    op("v", "crun", ["cnt", "keep"], v.tensor_tensor_scan, out=T.crun[0:1, :], data0=T.keep[0:1, :], data1=T.ps1[0:1, 0:128],
       initial=0.0, op0=A.mult, op1=A.add)
    op("v", "crow", ["crun"], v.tensor_copy, out=T.crow[0:1, :], in_=T.crun[0:1, 15:128:16])
    dma("y", "cout", ["crow"], T.cnt[:], T.crow[0:1, :])
    R["finish"]()


def send_two(R, T, g, topo, core, name, parts):
    tr, total = [], 0
    for jobs, rsem in parts:
        for dst, out, src, eng in jobs:
            rid, pid = topo.addr(dst, core)
            tr.append(RemoteDMATransfer(dst_ids=[DstId(rid=rid, pnc=pid)], dma_engine_mask=sum(1 << e for e in eng),
                                        remote_sem=T.sem[rsem], src=src, dst=out))
            total += len(eng)
    t = R["tag"](name)
    t["n"] = total
    g.remote_dma_fused(tr, local_sem=T.sem[t["sem"]])
